import numpy as np
import ml_dtypes


def mxq(x, axis, fmt="e4m3"):
    dtype, down = {"e4m3": (ml_dtypes.float8_e4m3fn, 7), "e5m2": (ml_dtypes.float8_e5m2, 14)}[fmt]
    v = np.moveaxis(np.asarray(x, np.float32).astype(ml_dtypes.bfloat16).astype(np.float64), axis, -1)
    blocks = v.reshape(v.shape[:-1] + (-1, 32))
    amax = np.abs(blocks).max(-1, keepdims=True)
    byte = np.maximum(np.where(amax > 0, np.frexp(amax)[1] - 1 + 127, 0) - down, 1)
    scale = np.exp2(byte - 127.0)
    codes = (blocks / scale).astype(np.float32).astype(dtype).astype(np.float64)
    return np.moveaxis((codes * scale).reshape(v.shape), -1, axis)


WIDE = False


def mx_kscale(k):
    if not WIDE:
        return np.ones(k)
    levels = np.array([10, -10, 5, -5, 0])
    if k % 512:
        return np.exp2(np.random.permutation(np.resize(levels, k // 32))).repeat(32)
    a = np.empty((k // 512, 16))
    for p in range(k // 512):
        a[p, :8] = np.random.permutation(np.resize(levels, 8))
        for g in range(8):
            far = levels[np.abs(levels - a[p, g]) >= 10]
            a[p, g + 8] = far[np.random.randint(len(far))]
    return np.exp2(a.ravel()).repeat(32)


def f64(x):
    return np.asarray(x).astype(np.float64)


E2M1 = np.array([0.0, 0.5, 1.0, 1.5, 2.0, 3.0, 4.0, 6.0, -0.0, -0.5, -1.0, -1.5, -2.0, -3.0, -4.0, -6.0])


def pack_weight(w, fmt):
    k, n = w.shape
    w = f64(np.asarray(w, np.float32).astype(ml_dtypes.bfloat16)).reshape(k // 32, 32, n)
    amax = np.abs(w).max(1)
    if fmt == "e4m3":
        byte = np.frexp(amax)[1] - 1 + 127 - 7
    else:
        mant, ex = np.frexp(amax / 6.0)
        byte = np.where(mant > 0.5, ex, ex - 1) + 127
    byte = np.clip(np.where(amax > 0, byte, 1), 1, 254)
    scaled = (w * np.exp2(127.0 - byte)[:, None, :]).reshape(k, n).astype(np.float32)
    by_word = np.ascontiguousarray(scaled.reshape(k // 512, 128, 4, n).transpose(0, 1, 3, 2))
    if fmt == "e4m3":
        words = by_word.astype(ml_dtypes.float8_e4m3fn).view(np.uint8)
    else:
        c = by_word.astype(ml_dtypes.float4_e2m1fn).view(np.uint8) & 0xF
        words = (c[..., 0::2] | (c[..., 1::2] << 4)).reshape(k // 512, 128, 2 * n)
    return np.ascontiguousarray(words), np.ascontiguousarray(byte.astype(np.uint8).reshape(k // 512, 16, n))


def unpack_weight(words, scales, fmt):
    g, _, n = scales.shape
    words = np.ascontiguousarray(words).reshape(g, 128, n, -1)
    if fmt == "e4m3":
        vals = words.view(ml_dtypes.float8_e4m3fn).astype(np.float64)
    else:
        nib = np.empty((g, 128, n, 4), np.uint8)
        nib[..., 0::2] = words & 0xF
        nib[..., 1::2] = words >> 4
        vals = E2M1[nib]
    vals = vals * np.repeat(np.exp2(scales.astype(np.float64) - 127.0), 8, axis=1)[..., None]
    return vals.transpose(0, 1, 3, 2).reshape(g * 512, n)


K, L, Q, I = 512, 1024, 512, 1024


def setup_inputs():
    n = np.random.standard_normal
    fk = mx_kscale(K)
    fl = mx_kscale(L)
    qap = pack_weight(n((K, Q)) * np.random.uniform(0.02, 0.1, (1, Q)) * fk[:, None], "e4m3")
    qbp = pack_weight(n((L, Q)) * np.random.uniform(0.01, 0.05, (1, Q)) * fl[:, None], "e2m1")
    kbp = pack_weight(n((L, I)) / fl[:, None], "e4m3")
    return {
        "qa_words": qap[0],
        "qa_scales": qap[1],
        "ka": (n((K, I)) / fk[:, None]).astype(np.float32),
        "qb_words": qbp[0],
        "qb_scales": qbp[1],
        "kb_words": kbp[0],
        "kb_scales": kbp[1],
        "gn": (np.random.uniform(0.5, 2.0, (1, I))).astype(np.float32),
        "bi": (np.random.uniform(-0.5, 0.5, (1, I))).astype(np.float32),
    }


def reference(qa_words, qa_scales, ka, qb_words, qb_scales, kb_words, kb_scales, gn, bi):
    qau = unpack_weight(qa_words, qa_scales, "e4m3")
    qbu = unpack_weight(qb_words, qb_scales, "e2m1")
    kbu = unpack_weight(kb_words, kb_scales, "e4m3")
    kaq = mxq(f64(ka), 0, "e4m3")
    a = qau.T @ kaq + qbu.T @ kbu
    d = a - np.mean(a, axis=1, keepdims=True)
    y = d / np.sqrt(np.mean(np.square(d), axis=1, keepdims=True) + 0.02) * f64(gn) + f64(bi)
    return y

@@ -1,0 +1,316 @@
+from contextlib import ExitStack
+
+import concourse.mybir as mybir
+from concourse.masks import make_identity
+
+K, L, Q, I = 512, 1024, 512, 1024
+FLOPS = 2 * Q * I * (K + L)
+
+F32 = mybir.dt.float32
+BF16 = mybir.dt.bfloat16
+I32 = mybir.dt.int32
+U32 = mybir.dt.uint32
+U8 = mybir.dt.uint8
+FP8X4 = mybir.dt.float8_e4m3fn_x4
+FP4X4 = mybir.dt.float4_e2m1fn_x4
+ACT = mybir.ActivationFunctionType
+ALU = mybir.AluOpType
+
+P = 128
+HALF = 512
+QUARTER = 256
+ROW_TILES = Q // P
+L_PASSES = L // 512
+EPS = 0.02
+GP_COLS = (512, 256, 128, 128)
+
+
+def tile_mix_scores_of_two_sources_levelled_kernel(
+    tc, qa_words, qa_scales, ka, qb_words, qb_scales, kb_words, kb_scales, gn, bi, out
+):
+    nc = tc.nc
+    with ExitStack() as ctx:
+        sb = ctx.enter_context(tc.tile_pool(name="sb", bufs=1))
+        ps = ctx.enter_context(tc.psum_pool(name="ps", bufs=1))
+        ctx.enter_context(tc.manual_schedule())
+
+        def tile(name, shape, dtype):
+            return sb.tile(shape, dtype, name=name, align_bytes=64)
+
+        def bank(name, tag):
+            return ps.tile([P, HALF], F32, name=name, tag=tag)
+
+        def halves(h):
+            return slice(h * HALF, (h + 1) * HALF)
+
+        ident = tile("ident", [P, P], F32)
+
+        kb_plane = tile("kb_plane", [P, L_PASSES, I], U8)
+        qb_plane = tile("qb_plane", [P, L_PASSES, Q], U8)
+        qa_plane = tile("qa_plane", [P, 1, Q], U8)
+        for plane in (kb_plane, qb_plane, qa_plane):
+            nc.vector.memset(plane[:].bitcast(I32), 0)
+        stats = [tile("stats%d" % j, [P, 12], F32) for j in range(ROW_TILES)]
+        for j in range(1, ROW_TILES):
+            nc.vector.memset(stats[j][:], float(HALF))
+        warm = tile("warm", [P, 1], F32)
+        nc.vector.memset(warm[:], 1.0)
+
+        def load_plane(engine, plane, scales):
+            for r in range(4):
+                engine.dma_start(
+                    out=plane[32 * r : 32 * r + 4].bitcast(I32),
+                    in_=scales[:, 4 * r : 4 * r + 4, :].rearrange("g s n -> s g n").bitcast(I32),
+                )
+
+        def load_columns(engine, name, vec):
+            cols = tile(name, [P, I // P], F32)
+            with nc.allow_non_contiguous_dma(reason="one value of a short vector to each partition"):
+                engine.dma_start(out=cols[:], in_=vec.rearrange("o (c p) -> p (o c)", p=P))
+            return cols
+
+        def load_kb(h):
+            t = tile("kb%d" % h, [P, L_PASSES, 4 * HALF], U8)
+            src = kb_words.rearrange("g p n t -> p g (n t)")[:, :, 4 * HALF * h : 4 * HALF * (h + 1)]
+            nc.sync.dma_start(out=t[:].bitcast(I32), in_=src.bitcast(I32))
+            return t
+
+        def load_ka(h):
+            t = tile("ka%d" % h, [P, 4, HALF], F32)
+            nc.sync.dma_start(out=t[:], in_=ka.rearrange("(p t) i -> p t i", t=4)[:, :, halves(h)])
+            return t
+
+        gn_cols = load_columns(nc.scalar, "gn_cols", gn)
+        make_identity(nc, ident[:])
+        bi_cols = load_columns(nc.gpsimd, "bi_cols", bi)
+        qb = tile("qb", [P, L_PASSES, 2 * Q], U8)
+        nc.sync.dma_start(out=qb[:].bitcast(I32), in_=qb_words.rearrange("g p n -> p g n").bitcast(I32))
+        load_plane(nc.sync, kb_plane, kb_scales)
+        kb = [load_kb(0)]
+        qa = tile("qa", [P, 4 * Q], U8)
+        nc.sync.dma_start(out=qa[:].bitcast(I32), in_=qa_words[0].rearrange("p n t -> p (n t)").bitcast(I32))
+        load_plane(nc.sync, qb_plane, qb_scales)
+        ka_raw = [load_ka(0)]
+        load_plane(nc.sync, qa_plane, qa_scales)
+        ka_raw.append(load_ka(1))
+        kb.append(load_kb(1))
+
+        warm_out = tile("warm_out", [P, 1], F32)
+        nc.scalar.activation(out=warm_out[:], in_=warm[:], func=ACT.Abs_reciprocal_sqrt)
+
+        def spread(cols, h, dst):
+            for c in range(4):
+                nc.tensor.transpose(
+                    dst[:, c * P : (c + 1) * P],
+                    cols[:, 4 * h + c : 4 * h + c + 1].to_broadcast([P, P]),
+                    ident[:],
+                )
+
+        gn_sb = tile("gn_sb", [P, I], F32)
+        for h in range(2):
+            b = bank("gn_ps%d" % h, "bank%d" % (4 + h))
+            spread(gn_cols, h, b)
+            nc.scalar.copy(out=gn_sb[:, halves(h)], in_=b[:])
+
+        ka_codes = [tile("ka_codes%d" % h, [P, HALF], U32) for h in range(2)]
+        ka_plane = [tile("ka_plane%d" % h, [P, HALF], U8) for h in range(2)]
+        grouped = {}
+
+        def interleave(h, u):
+            g = tile("grouped%d%d" % (h, u), [P, QUARTER, 4], BF16)
+            grouped[h, u] = g
+            raw = ka_raw[h][:, :, u * QUARTER : (u + 1) * QUARTER]
+            dst = g[:].rearrange("p (c n) t -> p c t n", n=4)
+            src = raw.rearrange("p t (c n) -> p c t n", n=4)
+            if u == 1:
+                nc.scalar.copy(out=dst, in_=src)
+            elif h == 0:
+                nc.vector.tensor_copy(out=dst, in_=src)
+            else:
+                nc.gpsimd.tensor_scalar(
+                    out=g[:], in0=raw.rearrange("p t n -> p n t"), scalar1=1.0, scalar2=0.0, op0=ALU.mult, op1=ALU.add
+                )
+
+        def quantise(h, u):
+            cols = slice(u * QUARTER, (u + 1) * QUARTER)
+            nc.vector.quantize_mx(
+                out=ka_codes[h][:, cols].bitcast(FP8X4),
+                scales=ka_plane[h][:, cols],
+                in_=grouped[h, u][:].rearrange("p n t -> p (n t)"),
+            )
+
+        acc = {}
+
+        def b_passes(j, h):
+            for g in range(L_PASSES):
+                nc.tensor.matmul_mx(
+                    out=acc[j, h][:],
+                    lhsT=qb[:, g, 2 * P * j : 2 * P * (j + 1)].bitcast(FP4X4),
+                    lhsT_scale=qb_plane[:, g, P * j : P * (j + 1)],
+                    rhs=kb[h][:, g, :].bitcast(FP8X4),
+                    rhs_scale=kb_plane[:, g, halves(h)],
+                    start=(g == 0),
+                    stop=False,
+                )
+
+        def a_pass(j, h):
+            nc.tensor.matmul_mx(
+                out=acc[j, h][:],
+                lhsT=qa[:, 4 * P * j : 4 * P * (j + 1)].bitcast(FP8X4),
+                lhsT_scale=qa_plane[:, 0, P * j : P * (j + 1)],
+                rhs=ka_codes[h][:].bitcast(FP8X4),
+                rhs_scale=ka_plane[h][:],
+                start=False,
+                stop=True,
+            )
+
+        filled = [0] * ROW_TILES
+        places = {}
+
+        def stats_vector(j, h):
+            at = filled[j]
+            filled[j] = at + 6
+            nc.vector.bn_stats(out=stats[j][:, at : at + 6], in_=acc[j, h][:])
+
+        def mean_scalar(j, h):
+            at = filled[j]
+            filled[j] = at + 3
+            places[j, h] = at
+            unused = tile("unused_a%d%d" % (j, h), [P, HALF], BF16)
+            nc.scalar.activation(
+                out=unused[:], in_=acc[j, h][:], func=ACT.Identity, scale=1.0 / HALF,
+                accum_out=stats[j][:, at + 1 : at + 2],
+            )
+
+        def spread_scalar(j, h):
+            at = places[j, h]
+            unused = tile("unused_b%d%d" % (j, h), [P, HALF], BF16)
+            nc.scalar.activation(
+                out=unused[:], in_=acc[j, h][:], func=ACT.Square, scale=-1.0,
+                bias=stats[j][:, at + 1 : at + 2], accum_out=stats[j][:, at + 2 : at + 3],
+            )
+
+        for j in range(ROW_TILES):
+            acc[j, 0] = bank("acc%d0" % j, "bank%d" % j)
+            b_passes(j, 0)
+
+        interleave(0, 0)
+        interleave(0, 1)
+        quantise(0, 0)
+        quantise(0, 1)
+        for j in range(ROW_TILES):
+            a_pass(j, 0)
+
+        bi_sb = tile("bi_sb", [P, HALF], F32)
+        b = bank("bi_first", "bank6")
+        spread(bi_cols, 0, b)
+        bi_ps = {1: bank("bi_ps1", "bank7")}
+        spread(bi_cols, 1, bi_ps[1])
+
+        interleave(1, 0)
+        interleave(1, 1)
+        nc.scalar.copy(out=bi_sb[:], in_=b[:])
+        for j in range(ROW_TILES):
+            stats_vector(j, 0)
+        quantise(1, 0)
+        quantise(1, 1)
+
+        for j in range(2):
+            acc[j, 1] = bank("acc%d1" % j, "bank%d" % (4 + j))
+            b_passes(j, 1)
+        for j in range(2):
+            a_pass(j, 1)
+        acc[2, 1] = bank("acc21", "bank6")
+        b_passes(2, 1)
+        a_pass(2, 1)
+
+        mv = [tile("mv%d" % j, [P, 2], F32) for j in range(ROW_TILES)]
+        rstd = [tile("rstd%d" % j, [P, 1], F32) for j in range(ROW_TILES)]
+        res = [tile("res%d" % j, [P, I], F32) for j in range(ROW_TILES)]
+        centred = {}
+        levelled = {}
+
+        def aggregate(j):
+            nc.vector.bn_aggr(out=mv[j][:], in_=stats[j][:, : filled[j]])
+
+        neg_mean = [tile("neg_mean%d" % j, [P, 1], F32) for j in range(ROW_TILES)]
+        shift = [tile("shift%d" % j, [P, 1], F32) for j in range(ROW_TILES)]
+
+        def inverse_spread(j):
+            nc.scalar.activation(out=rstd[j][:], in_=mv[j][:, 1:2], func=ACT.Abs_reciprocal_sqrt, bias=EPS)
+            nc.scalar.activation(out=neg_mean[j][:], in_=mv[j][:, 0:1], func=ACT.Identity, scale=-1.0)
+
+        def make_shift(j):
+            nc.scalar.activation(out=shift[j][:], in_=neg_mean[j][:], func=ACT.Identity, scale=rstd[j][:])
+
+        def level(j):
+            w = GP_COLS[j]
+            levelled[j] = tile("levelled%d" % j, [P, w], F32)
+            nc.scalar.activation(
+                out=levelled[j][:], in_=acc[j, 0][:, :w], func=ACT.Identity, scale=rstd[j][:], bias=shift[j][:]
+            )
+
+        def finish_gpsimd(j):
+            w = GP_COLS[j]
+            gained = tile("gained%d" % j, [P, w], F32)
+            nc.gpsimd.tensor_tensor(out=gained[:], in0=levelled[j][:], in1=gn_sb[:, :w], op=ALU.mult)
+            nc.gpsimd.tensor_tensor(out=res[j][:, :w], in0=gained[:], in1=bi_sb[:, :w], op=ALU.add)
+
+        def centre(j, h):
+            lo = GP_COLS[j] if h == 0 else 0
+            centred[j, h] = tile("centred%d%d" % (j, h), [P, HALF - lo], F32)
+            nc.vector.scalar_tensor_tensor(
+                out=centred[j, h][:], in0=acc[j, h][:, lo:], scalar=mv[j][:, 0:1],
+                in1=gn_sb[:, h * HALF + lo : (h + 1) * HALF], op0=ALU.subtract, op1=ALU.mult,
+            )
+
+        def finish_vector(j, h):
+            lo = GP_COLS[j] if h == 0 else 0
+            nc.vector.scalar_tensor_tensor(
+                out=res[j][:, h * HALF + lo : (h + 1) * HALF], in0=centred[j, h][:], scalar=rstd[j][:],
+                in1=bi_ps[h][:, lo:], op0=ALU.mult, op1=ALU.add,
+            )
+
+        def store(j, lo, hi):
+            nc.sync.dma_start(out=out[j * P : (j + 1) * P, lo:hi], in_=res[j][:, lo:hi])
+
+        stats_vector(0, 1)
+        mean_scalar(1, 1)
+        aggregate(0)
+        inverse_spread(0)
+        spread_scalar(1, 1)
+        make_shift(0)
+        centre(0, 1)
+        acc[3, 1] = bank("acc31", "bank4")
+        b_passes(3, 1)
+        a_pass(3, 1)
+        level(0)
+        bi_ps[0] = bank("bi_ps0", "bank0")
+        spread(bi_cols, 0, bi_ps[0])
+        finish_gpsimd(0)
+        aggregate(1)
+        finish_vector(0, 1)
+        store(0, HALF, I)
+        for j in range(1, ROW_TILES):
+            last = j == ROW_TILES - 1
+            inverse_spread(j)
+            centre(j, 0)
+            centre(j, 1)
+            if not last:
+                mean_scalar(j + 1, 1)
+            make_shift(j)
+            if not last:
+                spread_scalar(j + 1, 1)
+            level(j)
+            finish_gpsimd(j)
+            finish_vector(j, 1)
+            if last:
+                store(j - 1, 0, GP_COLS[j - 1])
+                store(j, HALF, I)
+            finish_vector(j, 0)
+            if not last:
+                aggregate(j + 1)
+                store(j, GP_COLS[j], I)
+                store(j - 1, 0, GP_COLS[j - 1])
+            else:
+                store(j, 0, HALF)

@@ -22,7 +22,7 @@ QUARTER = 256
 ROW_TILES = Q // P
 L_PASSES = L // 512
 EPS = 0.02
-GP_COLS = (512, 256, 128, 128)
+GP_COLS = (512, 256, 256, 128)
 
 
 def tile_mix_scores_of_two_sources_levelled_kernel(
@@ -45,10 +45,13 @@ def tile_mix_scores_of_two_sources_levelled_kernel(
 
         ident = tile("ident", [P, P], F32)
 
+        rows = tile("rows", [P, P], F32)
         kb_plane = tile("kb_plane", [P, L_PASSES, I], U8)
         qb_plane = tile("qb_plane", [P, L_PASSES, Q], U8)
         qa_plane = tile("qa_plane", [P, 1, Q], U8)
-        for plane in (kb_plane, qb_plane, qa_plane):
+        nc.vector.memset(kb_plane[:].bitcast(I32), 0)
+        nc.vector.memset(rows[:], 0.0)
+        for plane in (qb_plane, qa_plane):
             nc.vector.memset(plane[:].bitcast(I32), 0)
         stats = [tile("stats%d" % j, [P, 12], F32) for j in range(ROW_TILES)]
         for j in range(1, ROW_TILES):
@@ -59,15 +62,9 @@ def tile_mix_scores_of_two_sources_levelled_kernel(
         def load_plane(engine, plane, scales):
             for r in range(4):
                 engine.dma_start(
-                    out=plane[32 * r : 32 * r + 4].bitcast(I32),
-                    in_=scales[:, 4 * r : 4 * r + 4, :].rearrange("g s n -> s g n").bitcast(I32),
+                    out=plane[r:P:32].bitcast(I32),
+                    in_=scales[:, r:16:4, :].rearrange("g s n -> s g n").bitcast(I32),
                 )
-
-        def load_columns(engine, name, vec):
-            cols = tile(name, [P, I // P], F32)
-            with nc.allow_non_contiguous_dma(reason="one value of a short vector to each partition"):
-                engine.dma_start(out=cols[:], in_=vec.rearrange("o (c p) -> p (o c)", p=P))
-            return cols
 
         def load_kb(h):
             t = tile("kb%d" % h, [P, L_PASSES, 4 * HALF], U8)
@@ -75,14 +72,15 @@ def tile_mix_scores_of_two_sources_levelled_kernel(
             nc.sync.dma_start(out=t[:].bitcast(I32), in_=src.bitcast(I32))
             return t
 
-        def load_ka(h):
-            t = tile("ka%d" % h, [P, 4, HALF], F32)
-            nc.sync.dma_start(out=t[:], in_=ka.rearrange("(p t) i -> p t i", t=4)[:, :, halves(h)])
+        def load_ka(lo, hi):
+            t = tile("ka%d" % lo, [P, 4, hi - lo], F32)
+            nc.sync.dma_start(out=t[:], in_=ka.rearrange("(p t) i -> p t i", t=4)[:, :, lo:hi])
             return t
 
-        gn_cols = load_columns(nc.scalar, "gn_cols", gn)
+        blocks = I // P
+        nc.scalar.dma_start(out=rows[:blocks, :], in_=gn.rearrange("o (c n) -> (o c) n", n=P))
+        nc.scalar.dma_start(out=rows[blocks : 2 * blocks, :], in_=bi.rearrange("o (c n) -> (o c) n", n=P))
         make_identity(nc, ident[:])
-        bi_cols = load_columns(nc.gpsimd, "bi_cols", bi)
         qb = tile("qb", [P, L_PASSES, 2 * Q], U8)
         nc.sync.dma_start(out=qb[:].bitcast(I32), in_=qb_words.rearrange("g p n -> p g n").bitcast(I32))
         load_plane(nc.sync, kb_plane, kb_scales)
@@ -90,46 +88,46 @@ def tile_mix_scores_of_two_sources_levelled_kernel(
         qa = tile("qa", [P, 4 * Q], U8)
         nc.sync.dma_start(out=qa[:].bitcast(I32), in_=qa_words[0].rearrange("p n t -> p (n t)").bitcast(I32))
         load_plane(nc.sync, qb_plane, qb_scales)
-        ka_raw = [load_ka(0)]
+        ka_first = load_ka(0, HALF)
         load_plane(nc.sync, qa_plane, qa_scales)
-        ka_raw.append(load_ka(1))
+        ka_third = load_ka(HALF, HALF + QUARTER)
+        ka_last = load_ka(HALF + QUARTER, I)
         kb.append(load_kb(1))
 
         warm_out = tile("warm_out", [P, 1], F32)
         nc.scalar.activation(out=warm_out[:], in_=warm[:], func=ACT.Abs_reciprocal_sqrt)
 
-        def spread(cols, h, dst):
+        turned = bank("turned", "bank0")
+        nc.tensor.transpose(turned[:, :P], rows[:], ident[:])
+        cols = tile("cols", [P, 2 * blocks], F32)
+        nc.vector.tensor_copy(out=cols[:], in_=turned[:, : 2 * blocks])
+
+        def spread(first, dst):
             for c in range(4):
                 nc.tensor.transpose(
                     dst[:, c * P : (c + 1) * P],
-                    cols[:, 4 * h + c : 4 * h + c + 1].to_broadcast([P, P]),
+                    cols[:, first + c : first + c + 1].to_broadcast([P, P]),
                     ident[:],
                 )
 
         gn_sb = tile("gn_sb", [P, I], F32)
         for h in range(2):
             b = bank("gn_ps%d" % h, "bank%d" % (4 + h))
-            spread(gn_cols, h, b)
+            spread(4 * h, b)
             nc.scalar.copy(out=gn_sb[:, halves(h)], in_=b[:])
+        bi_sb = tile("bi_sb", [P, HALF], F32)
+        b = bank("bi_first", "bank6")
+        spread(blocks, b)
+        nc.scalar.copy(out=bi_sb[:], in_=b[:])
+        bi_ps = {1: bank("bi_ps1", "bank7")}
+        spread(blocks + 4, bi_ps[1])
 
         ka_codes = [tile("ka_codes%d" % h, [P, HALF], U32) for h in range(2)]
         ka_plane = [tile("ka_plane%d" % h, [P, HALF], U8) for h in range(2)]
-        grouped = {}
+        grouped = {(h, u): tile("grouped%d%d" % (h, u), [P, QUARTER, 4], BF16) for h in range(2) for u in range(2)}
 
-        def interleave(h, u):
-            g = tile("grouped%d%d" % (h, u), [P, QUARTER, 4], BF16)
-            grouped[h, u] = g
-            raw = ka_raw[h][:, :, u * QUARTER : (u + 1) * QUARTER]
-            dst = g[:].rearrange("p (c n) t -> p c t n", n=4)
-            src = raw.rearrange("p t (c n) -> p c t n", n=4)
-            if u == 1:
-                nc.scalar.copy(out=dst, in_=src)
-            elif h == 0:
-                nc.vector.tensor_copy(out=dst, in_=src)
-            else:
-                nc.gpsimd.tensor_scalar(
-                    out=g[:], in0=raw.rearrange("p t n -> p n t"), scalar1=1.0, scalar2=0.0, op0=ALU.mult, op1=ALU.add
-                )
+        def interleave(copy, dst, raw):
+            copy(out=dst.rearrange("p (c n) t -> p c t n", n=4), in_=raw.rearrange("p t (c n) -> p c t n", n=4))
 
         def quantise(h, u):
             cols = slice(u * QUARTER, (u + 1) * QUARTER)
@@ -194,35 +192,30 @@ def tile_mix_scores_of_two_sources_levelled_kernel(
             acc[j, 0] = bank("acc%d0" % j, "bank%d" % j)
             b_passes(j, 0)
 
-        interleave(0, 0)
-        interleave(0, 1)
+        interleave(nc.vector.tensor_copy, grouped[0, 0][:], ka_first[:, :, :QUARTER])
+        interleave(nc.scalar.copy, grouped[0, 1][:], ka_first[:, :, QUARTER:])
         quantise(0, 0)
         quantise(0, 1)
         for j in range(ROW_TILES):
             a_pass(j, 0)
 
-        bi_sb = tile("bi_sb", [P, HALF], F32)
-        b = bank("bi_first", "bank6")
-        spread(bi_cols, 0, b)
-        bi_ps = {1: bank("bi_ps1", "bank7")}
-        spread(bi_cols, 1, bi_ps[1])
-
-        interleave(1, 0)
-        interleave(1, 1)
-        nc.scalar.copy(out=bi_sb[:], in_=b[:])
-        for j in range(ROW_TILES):
-            stats_vector(j, 0)
+        nc.gpsimd.tensor_scalar(
+            out=grouped[1, 0][:], in0=ka_third[:].rearrange("p t n -> p n t"),
+            scalar1=1.0, scalar2=0.0, op0=ALU.mult, op1=ALU.add,
+        )
+        stats_vector(0, 0)
+        interleave(nc.vector.tensor_copy, grouped[1, 1][:, :P, :], ka_last[:, :, :P])
+        interleave(nc.scalar.copy, grouped[1, 1][:, P:, :], ka_last[:, :, P:])
         quantise(1, 0)
         quantise(1, 1)
+        stats_vector(1, 0)
+        mean_scalar(3, 0)
+        spread_scalar(3, 0)
 
-        for j in range(2):
+        for j in range(3):
             acc[j, 1] = bank("acc%d1" % j, "bank%d" % (4 + j))
             b_passes(j, 1)
-        for j in range(2):
             a_pass(j, 1)
-        acc[2, 1] = bank("acc21", "bank6")
-        b_passes(2, 1)
-        a_pass(2, 1)
 
         mv = [tile("mv%d" % j, [P, 2], F32) for j in range(ROW_TILES)]
         rstd = [tile("rstd%d" % j, [P, 1], F32) for j in range(ROW_TILES)]
@@ -277,6 +270,7 @@ def tile_mix_scores_of_two_sources_levelled_kernel(
         stats_vector(0, 1)
         mean_scalar(1, 1)
         aggregate(0)
+        stats_vector(2, 0)
         inverse_spread(0)
         spread_scalar(1, 1)
         make_shift(0)
@@ -286,31 +280,32 @@ def tile_mix_scores_of_two_sources_levelled_kernel(
         a_pass(3, 1)
         level(0)
         bi_ps[0] = bank("bi_ps0", "bank0")
-        spread(bi_cols, 0, bi_ps[0])
+        spread(blocks, bi_ps[0])
         finish_gpsimd(0)
         aggregate(1)
         finish_vector(0, 1)
         store(0, HALF, I)
         for j in range(1, ROW_TILES):
             last = j == ROW_TILES - 1
+            if not last:
+                mean_scalar(j + 1, 1)
             inverse_spread(j)
             centre(j, 0)
             centre(j, 1)
             if not last:
-                mean_scalar(j + 1, 1)
-            make_shift(j)
-            if not last:
                 spread_scalar(j + 1, 1)
+            make_shift(j)
             level(j)
             finish_gpsimd(j)
             finish_vector(j, 1)
             if last:
                 store(j - 1, 0, GP_COLS[j - 1])
                 store(j, HALF, I)
-            finish_vector(j, 0)
-            if not last:
+            else:
                 aggregate(j + 1)
+            finish_vector(j, 0)
+            if last:
+                store(j, 0, HALF)
+            else:
                 store(j, GP_COLS[j], I)
                 store(j - 1, 0, GP_COLS[j - 1])
-            else:
-                store(j, 0, HALF)

@@ -22,7 +22,8 @@ QUARTER = 256
 ROW_TILES = Q // P
 L_PASSES = L // 512
 EPS = 0.02
-GP_COLS = (512, 256, 256, 128)
+SCALAR_COLS = 64
+QA_ROW = 4
 
 
 def tile_mix_scores_of_two_sources_levelled_kernel(
@@ -45,12 +46,10 @@ def tile_mix_scores_of_two_sources_levelled_kernel(
 
         ident = tile("ident", [P, P], F32)
 
-        rows = tile("rows", [P, P], F32)
         kb_plane = tile("kb_plane", [P, L_PASSES, I], U8)
         qb_plane = tile("qb_plane", [P, L_PASSES, Q], U8)
         qa_plane = tile("qa_plane", [P, 1, Q], U8)
         nc.vector.memset(kb_plane[:].bitcast(I32), 0)
-        nc.vector.memset(rows[:], 0.0)
         for plane in (qb_plane, qa_plane):
             nc.vector.memset(plane[:].bitcast(I32), 0)
         stats = [tile("stats%d" % j, [P, 12], F32) for j in range(ROW_TILES)]
@@ -59,10 +58,10 @@ def tile_mix_scores_of_two_sources_levelled_kernel(
         warm = tile("warm", [P, 1], F32)
         nc.vector.memset(warm[:], 1.0)
 
-        def load_plane(engine, plane, scales):
+        def load_plane(engine, plane, scales, first=0):
             for r in range(4):
                 engine.dma_start(
-                    out=plane[r:P:32].bitcast(I32),
+                    out=plane[first + r : P : 32].bitcast(I32),
                     in_=scales[:, r:16:4, :].rearrange("g s n -> s g n").bitcast(I32),
                 )
 
@@ -78,8 +77,10 @@ def tile_mix_scores_of_two_sources_levelled_kernel(
             return t
 
         blocks = I // P
-        nc.scalar.dma_start(out=rows[:blocks, :], in_=gn.rearrange("o (c n) -> (o c) n", n=P))
-        nc.scalar.dma_start(out=rows[blocks : 2 * blocks, :], in_=bi.rearrange("o (c n) -> (o c) n", n=P))
+        gn_cols = tile("gn_cols", [P, blocks], F32)
+        bi_cols = tile("bi_cols", [P, blocks], F32)
+        nc.scalar.dma_start(out=gn_cols[:], in_=gn.rearrange("o (p c) -> (o p) c", p=P))
+        nc.scalar.dma_start(out=bi_cols[:], in_=bi.rearrange("o (p c) -> (o p) c", p=P))
         make_identity(nc, ident[:])
         qb = tile("qb", [P, L_PASSES, 2 * Q], U8)
         nc.sync.dma_start(out=qb[:].bitcast(I32), in_=qb_words.rearrange("g p n -> p g n").bitcast(I32))
@@ -89,7 +90,7 @@ def tile_mix_scores_of_two_sources_levelled_kernel(
         nc.sync.dma_start(out=qa[:].bitcast(I32), in_=qa_words[0].rearrange("p n t -> p (n t)").bitcast(I32))
         load_plane(nc.sync, qb_plane, qb_scales)
         ka_first = load_ka(0, HALF)
-        load_plane(nc.sync, qa_plane, qa_scales)
+        load_plane(nc.sync, qa_plane, qa_scales, QA_ROW)
         ka_third = load_ka(HALF, HALF + QUARTER)
         ka_last = load_ka(HALF + QUARTER, I)
         kb.append(load_kb(1))
@@ -97,30 +98,24 @@ def tile_mix_scores_of_two_sources_levelled_kernel(
         warm_out = tile("warm_out", [P, 1], F32)
         nc.scalar.activation(out=warm_out[:], in_=warm[:], func=ACT.Abs_reciprocal_sqrt)
 
-        turned = bank("turned", "bank0")
-        nc.tensor.transpose(turned[:, :P], rows[:], ident[:])
-        cols = tile("cols", [P, 2 * blocks], F32)
-        nc.vector.tensor_copy(out=cols[:], in_=turned[:, : 2 * blocks])
-
-        def spread(first, dst):
-            for c in range(4):
-                nc.tensor.transpose(
-                    dst[:, c * P : (c + 1) * P],
-                    cols[:, first + c : first + c + 1].to_broadcast([P, P]),
-                    ident[:],
+        def spread(name, cols, first_bank):
+            full = tile(name, [P, I], F32)
+            for u in range(2):
+                b = bank("%s%d" % (name, u), "bank%d" % (first_bank + u))
+                for c in range(4):
+                    nc.tensor.transpose(
+                        b[:, c * P : (c + 1) * P],
+                        cols[:, 4 * u + c : 4 * u + c + 1].to_broadcast([P, P]),
+                        ident[:],
+                    )
+                nc.scalar.copy(
+                    out=full[:].rearrange("p (n c) -> p n c", c=blocks)[:, :, 4 * u : 4 * u + 4],
+                    in_=b[:].rearrange("p (c n) -> p n c", c=4),
                 )
+            return full
 
-        gn_sb = tile("gn_sb", [P, I], F32)
-        for h in range(2):
-            b = bank("gn_ps%d" % h, "bank%d" % (4 + h))
-            spread(4 * h, b)
-            nc.scalar.copy(out=gn_sb[:, halves(h)], in_=b[:])
-        bi_sb = tile("bi_sb", [P, HALF], F32)
-        b = bank("bi_first", "bank6")
-        spread(blocks, b)
-        nc.scalar.copy(out=bi_sb[:], in_=b[:])
-        bi_ps = {1: bank("bi_ps1", "bank7")}
-        spread(blocks + 4, bi_ps[1])
+        gn_sb = spread("gn_sb", gn_cols, 4)
+        bi_sb = spread("bi_sb", bi_cols, 6)
 
         ka_codes = [tile("ka_codes%d" % h, [P, HALF], U32) for h in range(2)]
         ka_plane = [tile("ka_plane%d" % h, [P, HALF], U8) for h in range(2)]
@@ -155,7 +150,7 @@ def tile_mix_scores_of_two_sources_levelled_kernel(
             nc.tensor.matmul_mx(
                 out=acc[j, h][:],
                 lhsT=qa[:, 4 * P * j : 4 * P * (j + 1)].bitcast(FP8X4),
-                lhsT_scale=qa_plane[:, 0, P * j : P * (j + 1)],
+                lhsT_scale=qa_plane[QA_ROW:, 0, P * j : P * (j + 1)],
                 rhs=ka_codes[h][:].bitcast(FP8X4),
                 rhs_scale=ka_plane[h][:],
                 start=False,
@@ -199,113 +194,64 @@ def tile_mix_scores_of_two_sources_levelled_kernel(
         for j in range(ROW_TILES):
             a_pass(j, 0)
 
-        nc.gpsimd.tensor_scalar(
-            out=grouped[1, 0][:], in0=ka_third[:].rearrange("p t n -> p n t"),
-            scalar1=1.0, scalar2=0.0, op0=ALU.mult, op1=ALU.add,
-        )
+        interleave(nc.scalar.copy, grouped[1, 0][:], ka_third[:])
         stats_vector(0, 0)
-        interleave(nc.vector.tensor_copy, grouped[1, 1][:, :P, :], ka_last[:, :, :P])
-        interleave(nc.scalar.copy, grouped[1, 1][:, P:, :], ka_last[:, :, P:])
+        cut = QUARTER - SCALAR_COLS
+        interleave(nc.vector.tensor_copy, grouped[1, 1][:, :cut, :], ka_last[:, :, :cut])
+        interleave(nc.scalar.copy, grouped[1, 1][:, cut:, :], ka_last[:, :, cut:])
         quantise(1, 0)
         quantise(1, 1)
         stats_vector(1, 0)
-        mean_scalar(3, 0)
-        spread_scalar(3, 0)
+        mean_scalar(2, 0)
+        spread_scalar(2, 0)
 
-        for j in range(3):
+        for j in range(ROW_TILES):
             acc[j, 1] = bank("acc%d1" % j, "bank%d" % (4 + j))
             b_passes(j, 1)
             a_pass(j, 1)
 
         mv = [tile("mv%d" % j, [P, 2], F32) for j in range(ROW_TILES)]
         rstd = [tile("rstd%d" % j, [P, 1], F32) for j in range(ROW_TILES)]
+        centred = [tile("centred%d" % j, [P, I], F32) for j in range(ROW_TILES)]
         res = [tile("res%d" % j, [P, I], F32) for j in range(ROW_TILES)]
-        centred = {}
-        levelled = {}
 
         def aggregate(j):
             nc.vector.bn_aggr(out=mv[j][:], in_=stats[j][:, : filled[j]])
 
-        neg_mean = [tile("neg_mean%d" % j, [P, 1], F32) for j in range(ROW_TILES)]
-        shift = [tile("shift%d" % j, [P, 1], F32) for j in range(ROW_TILES)]
-
         def inverse_spread(j):
             nc.scalar.activation(out=rstd[j][:], in_=mv[j][:, 1:2], func=ACT.Abs_reciprocal_sqrt, bias=EPS)
-            nc.scalar.activation(out=neg_mean[j][:], in_=mv[j][:, 0:1], func=ACT.Identity, scale=-1.0)
-
-        def make_shift(j):
-            nc.scalar.activation(out=shift[j][:], in_=neg_mean[j][:], func=ACT.Identity, scale=rstd[j][:])
-
-        def level(j):
-            w = GP_COLS[j]
-            levelled[j] = tile("levelled%d" % j, [P, w], F32)
-            nc.scalar.activation(
-                out=levelled[j][:], in_=acc[j, 0][:, :w], func=ACT.Identity, scale=rstd[j][:], bias=shift[j][:]
-            )
-
-        def finish_gpsimd(j):
-            w = GP_COLS[j]
-            gained = tile("gained%d" % j, [P, w], F32)
-            nc.gpsimd.tensor_tensor(out=gained[:], in0=levelled[j][:], in1=gn_sb[:, :w], op=ALU.mult)
-            nc.gpsimd.tensor_tensor(out=res[j][:, :w], in0=gained[:], in1=bi_sb[:, :w], op=ALU.add)
 
         def centre(j, h):
-            lo = GP_COLS[j] if h == 0 else 0
-            centred[j, h] = tile("centred%d%d" % (j, h), [P, HALF - lo], F32)
             nc.vector.scalar_tensor_tensor(
-                out=centred[j, h][:], in0=acc[j, h][:, lo:], scalar=mv[j][:, 0:1],
-                in1=gn_sb[:, h * HALF + lo : (h + 1) * HALF], op0=ALU.subtract, op1=ALU.mult,
+                out=centred[j][:, halves(h)], in0=acc[j, h][:], scalar=mv[j][:, 0:1],
+                in1=gn_sb[:, halves(h)], op0=ALU.subtract, op1=ALU.mult,
             )
 
-        def finish_vector(j, h):
-            lo = GP_COLS[j] if h == 0 else 0
+        def finish(j, h):
             nc.vector.scalar_tensor_tensor(
-                out=res[j][:, h * HALF + lo : (h + 1) * HALF], in0=centred[j, h][:], scalar=rstd[j][:],
-                in1=bi_ps[h][:, lo:], op0=ALU.mult, op1=ALU.add,
+                out=res[j][:, halves(h)], in0=centred[j][:, halves(h)], scalar=rstd[j][:],
+                in1=bi_sb[:, halves(h)], op0=ALU.mult, op1=ALU.add,
             )
-
-        def store(j, lo, hi):
-            nc.sync.dma_start(out=out[j * P : (j + 1) * P, lo:hi], in_=res[j][:, lo:hi])
+            nc.sync.dma_start(out=out[j * P : (j + 1) * P, halves(h)], in_=res[j][:, halves(h)])
 
         stats_vector(0, 1)
         mean_scalar(1, 1)
         aggregate(0)
-        stats_vector(2, 0)
-        inverse_spread(0)
-        spread_scalar(1, 1)
-        make_shift(0)
-        centre(0, 1)
-        acc[3, 1] = bank("acc31", "bank4")
-        b_passes(3, 1)
-        a_pass(3, 1)
-        level(0)
-        bi_ps[0] = bank("bi_ps0", "bank0")
-        spread(blocks, bi_ps[0])
-        finish_gpsimd(0)
-        aggregate(1)
-        finish_vector(0, 1)
-        store(0, HALF, I)
-        for j in range(1, ROW_TILES):
-            last = j == ROW_TILES - 1
-            if not last:
-                mean_scalar(j + 1, 1)
+        for j in range(ROW_TILES):
             inverse_spread(j)
+            if j == 0:
+                spread_scalar(1, 1)
+                mean_scalar(2, 1)
+            elif j == 1:
+                spread_scalar(2, 1)
+                mean_scalar(3, 0)
+                spread_scalar(3, 0)
+                mean_scalar(3, 1)
+            elif j == 2:
+                spread_scalar(3, 1)
             centre(j, 0)
             centre(j, 1)
-            if not last:
-                spread_scalar(j + 1, 1)
-            make_shift(j)
-            level(j)
-            finish_gpsimd(j)
-            finish_vector(j, 1)
-            if last:
-                store(j - 1, 0, GP_COLS[j - 1])
-                store(j, HALF, I)
-            else:
+            finish(j, 0)
+            if j + 1 < ROW_TILES:
                 aggregate(j + 1)
-            finish_vector(j, 0)
-            if last:
-                store(j, 0, HALF)
-            else:
-                store(j, GP_COLS[j], I)
-                store(j - 1, 0, GP_COLS[j - 1])
+            finish(j, 1)

@@ -65,9 +65,22 @@ def tile_mix_scores_of_two_sources_levelled_kernel(
                     in_=scales[:, r:16:4, :].rearrange("g s n -> s g n").bitcast(I32),
                 )
 
-        def load_kb(h):
-            t = tile("kb%d" % h, [P, L_PASSES, 4 * HALF], U8)
-            src = kb_words.rearrange("g p n t -> p g (n t)")[:, :, 4 * HALF * h : 4 * HALF * (h + 1)]
+        def load_kb(h, first, count):
+            t = tile("kb%d%d" % (h, first), [P, count, 4 * HALF], U8)
+            src = kb_words.rearrange("g p n t -> p g (n t)")[:, first : first + count, 4 * HALF * h : 4 * HALF * (h + 1)]
+            nc.sync.dma_start(out=t[:].bitcast(I32), in_=src.bitcast(I32))
+            for g in range(count):
+                kb[h, first + g] = t[:, g, :]
+
+        def load_qb(v):
+            t = tile("qb%d" % v, [P, L_PASSES, Q], U8)
+            src = qb_words.rearrange("g p n -> p g n")[:, :, Q * v : Q * (v + 1)]
+            nc.sync.dma_start(out=t[:].bitcast(I32), in_=src.bitcast(I32))
+            return t
+
+        def load_qa(v):
+            t = tile("qa%d" % v, [P, 2 * Q], U8)
+            src = qa_words[0].rearrange("p n t -> p (n t)")[:, 2 * Q * v : 2 * Q * (v + 1)]
             nc.sync.dma_start(out=t[:].bitcast(I32), in_=src.bitcast(I32))
             return t
 
@@ -82,40 +95,45 @@ def tile_mix_scores_of_two_sources_levelled_kernel(
         nc.scalar.dma_start(out=gn_cols[:], in_=gn.rearrange("o (p c) -> (o p) c", p=P))
         nc.scalar.dma_start(out=bi_cols[:], in_=bi.rearrange("o (p c) -> (o p) c", p=P))
         make_identity(nc, ident[:])
-        qb = tile("qb", [P, L_PASSES, 2 * Q], U8)
-        nc.sync.dma_start(out=qb[:].bitcast(I32), in_=qb_words.rearrange("g p n -> p g n").bitcast(I32))
+        kb = {}
+        qb = [load_qb(0)]
+        load_kb(0, 0, L_PASSES)
         load_plane(nc.sync, kb_plane, kb_scales)
-        kb = [load_kb(0)]
-        qa = tile("qa", [P, 4 * Q], U8)
-        nc.sync.dma_start(out=qa[:].bitcast(I32), in_=qa_words[0].rearrange("p n t -> p (n t)").bitcast(I32))
-        load_plane(nc.sync, qb_plane, qb_scales)
         ka_first = load_ka(0, HALF)
-        load_plane(nc.sync, qa_plane, qa_scales, QA_ROW)
+        load_plane(nc.sync, qb_plane, qb_scales)
         ka_third = load_ka(HALF, HALF + QUARTER)
         ka_last = load_ka(HALF + QUARTER, I)
-        kb.append(load_kb(1))
+        qa = [load_qa(0)]
+        load_plane(nc.sync, qa_plane, qa_scales, QA_ROW)
+        load_kb(1, 0, 1)
+        load_kb(1, 1, 1)
+        qb.append(load_qb(1))
+        qa.append(load_qa(1))
 
         warm_out = tile("warm_out", [P, 1], F32)
         nc.scalar.activation(out=warm_out[:], in_=warm[:], func=ACT.Abs_reciprocal_sqrt)
 
         def spread(name, cols, first_bank):
+            banks = [bank("%s%d" % (name, u), "bank%d" % (first_bank + u)) for u in range(2)]
+            for c in range(blocks):
+                nc.tensor.transpose(
+                    banks[c // 4][:, (c % 4) * P : (c % 4 + 1) * P],
+                    cols[:, c : c + 1].to_broadcast([P, P]),
+                    ident[:],
+                )
+            return banks
+
+        def gather(name, banks):
             full = tile(name, [P, I], F32)
             for u in range(2):
-                b = bank("%s%d" % (name, u), "bank%d" % (first_bank + u))
-                for c in range(4):
-                    nc.tensor.transpose(
-                        b[:, c * P : (c + 1) * P],
-                        cols[:, 4 * u + c : 4 * u + c + 1].to_broadcast([P, P]),
-                        ident[:],
-                    )
                 nc.scalar.copy(
                     out=full[:].rearrange("p (n c) -> p n c", c=blocks)[:, :, 4 * u : 4 * u + 4],
-                    in_=b[:].rearrange("p (c n) -> p n c", c=4),
+                    in_=banks[u][:].rearrange("p (c n) -> p n c", c=4),
                 )
             return full
 
-        gn_sb = spread("gn_sb", gn_cols, 4)
-        bi_sb = spread("bi_sb", bi_cols, 6)
+        gn_sb = gather("gn_sb", spread("gn_ps", gn_cols, 2))
+        bi_sb = gather("bi_sb", spread("bi_ps", bi_cols, 6))
 
         ka_codes = [tile("ka_codes%d" % h, [P, HALF], U32) for h in range(2)]
         ka_plane = [tile("ka_plane%d" % h, [P, HALF], U8) for h in range(2)]
@@ -134,28 +152,37 @@ def tile_mix_scores_of_two_sources_levelled_kernel(
 
         acc = {}
 
-        def b_passes(j, h):
-            for g in range(L_PASSES):
-                nc.tensor.matmul_mx(
-                    out=acc[j, h][:],
-                    lhsT=qb[:, g, 2 * P * j : 2 * P * (j + 1)].bitcast(FP4X4),
-                    lhsT_scale=qb_plane[:, g, P * j : P * (j + 1)],
-                    rhs=kb[h][:, g, :].bitcast(FP8X4),
-                    rhs_scale=kb_plane[:, g, halves(h)],
-                    start=(g == 0),
-                    stop=False,
-                )
-
-        def a_pass(j, h):
+        def b_pass(j, h, g, start=False, stop=False):
             nc.tensor.matmul_mx(
                 out=acc[j, h][:],
-                lhsT=qa[:, 4 * P * j : 4 * P * (j + 1)].bitcast(FP8X4),
+                lhsT=qb[j // 2][:, g, 2 * P * (j % 2) : 2 * P * (j % 2 + 1)].bitcast(FP4X4),
+                lhsT_scale=qb_plane[:, g, P * j : P * (j + 1)],
+                rhs=kb[h, g].bitcast(FP8X4),
+                rhs_scale=kb_plane[:, g, halves(h)],
+                start=start,
+                stop=stop,
+            )
+
+        def a_pass(j, h, stop=False):
+            nc.tensor.matmul_mx(
+                out=acc[j, h][:],
+                lhsT=qa[j // 2][:, 4 * P * (j % 2) : 4 * P * (j % 2 + 1)].bitcast(FP8X4),
                 lhsT_scale=qa_plane[QA_ROW:, 0, P * j : P * (j + 1)],
                 rhs=ka_codes[h][:].bitcast(FP8X4),
                 rhs_scale=ka_plane[h][:],
                 start=False,
-                stop=True,
+                stop=stop,
             )
+
+        def scores(j, h):
+            acc[j, h] = bank("acc%d%d" % (j, h), "bank%d" % (4 * h + j))
+            b_pass(j, h, 0, start=True)
+            if h == 0:
+                b_pass(j, h, 1)
+                a_pass(j, h, stop=True)
+            else:
+                a_pass(j, h)
+                b_pass(j, h, 1, stop=True)
 
         filled = [0] * ROW_TILES
         places = {}
@@ -183,32 +210,33 @@ def tile_mix_scores_of_two_sources_levelled_kernel(
                 bias=stats[j][:, at + 1 : at + 2], accum_out=stats[j][:, at + 2 : at + 3],
             )
 
-        for j in range(ROW_TILES):
+        for j in range(2):
             acc[j, 0] = bank("acc%d0" % j, "bank%d" % j)
-            b_passes(j, 0)
+            b_pass(j, 0, 0, start=True)
+            b_pass(j, 0, 1)
 
         interleave(nc.vector.tensor_copy, grouped[0, 0][:], ka_first[:, :, :QUARTER])
         interleave(nc.scalar.copy, grouped[0, 1][:], ka_first[:, :, QUARTER:])
         quantise(0, 0)
         quantise(0, 1)
-        for j in range(ROW_TILES):
-            a_pass(j, 0)
+        for j in range(2):
+            a_pass(j, 0, stop=True)
 
         interleave(nc.scalar.copy, grouped[1, 0][:], ka_third[:])
-        stats_vector(0, 0)
         cut = QUARTER - SCALAR_COLS
         interleave(nc.vector.tensor_copy, grouped[1, 1][:, :cut, :], ka_last[:, :, :cut])
         interleave(nc.scalar.copy, grouped[1, 1][:, cut:, :], ka_last[:, :, cut:])
         quantise(1, 0)
         quantise(1, 1)
-        stats_vector(1, 0)
-        mean_scalar(2, 0)
-        spread_scalar(2, 0)
+        stats_vector(0, 0)
+        mean_scalar(1, 0)
+        spread_scalar(1, 0)
 
-        for j in range(ROW_TILES):
-            acc[j, 1] = bank("acc%d1" % j, "bank%d" % (4 + j))
-            b_passes(j, 1)
-            a_pass(j, 1)
+        scores(0, 1)
+        scores(1, 1)
+        for j in range(2, ROW_TILES):
+            scores(j, 0)
+            scores(j, 1)
 
         mv = [tile("mv%d" % j, [P, 2], F32) for j in range(ROW_TILES)]
         rstd = [tile("rstd%d" % j, [P, 1], F32) for j in range(ROW_TILES)]
@@ -221,37 +249,40 @@ def tile_mix_scores_of_two_sources_levelled_kernel(
         def inverse_spread(j):
             nc.scalar.activation(out=rstd[j][:], in_=mv[j][:, 1:2], func=ACT.Abs_reciprocal_sqrt, bias=EPS)
 
-        def centre(j, h):
+        def centre(j, lo, hi):
+            h = lo // HALF
             nc.vector.scalar_tensor_tensor(
-                out=centred[j][:, halves(h)], in0=acc[j, h][:], scalar=mv[j][:, 0:1],
-                in1=gn_sb[:, halves(h)], op0=ALU.subtract, op1=ALU.mult,
+                out=centred[j][:, lo:hi], in0=acc[j, h][:, lo - h * HALF : hi - h * HALF], scalar=mv[j][:, 0:1],
+                in1=gn_sb[:, lo:hi], op0=ALU.subtract, op1=ALU.mult,
             )
 
-        def finish(j, h):
+        def finish(j, lo, hi):
             nc.vector.scalar_tensor_tensor(
-                out=res[j][:, halves(h)], in0=centred[j][:, halves(h)], scalar=rstd[j][:],
-                in1=bi_sb[:, halves(h)], op0=ALU.mult, op1=ALU.add,
+                out=res[j][:, lo:hi], in0=centred[j][:, lo:hi], scalar=rstd[j][:],
+                in1=bi_sb[:, lo:hi], op0=ALU.mult, op1=ALU.add,
             )
-            nc.sync.dma_start(out=out[j * P : (j + 1) * P, halves(h)], in_=res[j][:, halves(h)])
+            nc.sync.dma_start(out=out[j * P : (j + 1) * P, lo:hi], in_=res[j][:, lo:hi])
 
         stats_vector(0, 1)
         mean_scalar(1, 1)
         aggregate(0)
         for j in range(ROW_TILES):
             inverse_spread(j)
-            if j == 0:
-                spread_scalar(1, 1)
-                mean_scalar(2, 1)
-            elif j == 1:
-                spread_scalar(2, 1)
-                mean_scalar(3, 0)
-                spread_scalar(3, 0)
-                mean_scalar(3, 1)
-            elif j == 2:
-                spread_scalar(3, 1)
-            centre(j, 0)
-            centre(j, 1)
-            finish(j, 0)
             if j + 1 < ROW_TILES:
+                spread_scalar(j + 1, 1)
+            if j + 2 < ROW_TILES:
+                mean_scalar(j + 2, 0)
+                spread_scalar(j + 2, 0)
+                mean_scalar(j + 2, 1)
+            centre(j, 0, HALF)
+            if j + 1 < ROW_TILES:
+                centre(j, HALF, I)
+                finish(j, 0, HALF)
                 aggregate(j + 1)
-            finish(j, 1)
+                finish(j, HALF, I)
+            else:
+                centre(j, HALF, HALF + QUARTER)
+                finish(j, 0, HALF)
+                centre(j, HALF + QUARTER, I)
+                finish(j, HALF, HALF + QUARTER)
+                finish(j, HALF + QUARTER, I)

@@ -104,7 +104,7 @@ def tile_mix_scores_of_two_sources_levelled_kernel(
         ka_third = load_ka(HALF, HALF + QUARTER)
         ka_last = load_ka(HALF + QUARTER, I)
         qa = [load_qa(0)]
-        load_plane(nc.sync, qa_plane, qa_scales, QA_ROW)
+        load_plane(nc.gpsimd, qa_plane, qa_scales, QA_ROW)
         load_kb(1, 0, 1)
         load_kb(1, 1, 1)
         qb.append(load_qb(1))
@@ -264,25 +264,29 @@ def tile_mix_scores_of_two_sources_levelled_kernel(
             nc.sync.dma_start(out=out[j * P : (j + 1) * P, lo:hi], in_=res[j][:, lo:hi])
 
         stats_vector(0, 1)
-        mean_scalar(1, 1)
         aggregate(0)
-        for j in range(ROW_TILES):
-            inverse_spread(j)
-            if j + 1 < ROW_TILES:
-                spread_scalar(j + 1, 1)
-            if j + 2 < ROW_TILES:
-                mean_scalar(j + 2, 0)
-                spread_scalar(j + 2, 0)
-                mean_scalar(j + 2, 1)
+        stats_vector(1, 1)
+        inverse_spread(0)
+        centre(0, 0, HALF)
+        aggregate(1)
+        mean_scalar(2, 0)
+        inverse_spread(1)
+        mean_scalar(2, 1)
+        spread_scalar(2, 0)
+        spread_scalar(2, 1)
+        centre(0, HALF, I)
+        finish(0, 0, HALF)
+        finish(0, HALF, I)
+        mean_scalar(3, 0)
+        mean_scalar(3, 1)
+        for j in range(1, ROW_TILES):
             centre(j, 0, HALF)
+            centre(j, HALF, I)
+            finish(j, 0, HALF)
+            if j == 2:
+                spread_scalar(3, 0)
+                spread_scalar(3, 1)
             if j + 1 < ROW_TILES:
-                centre(j, HALF, I)
-                finish(j, 0, HALF)
                 aggregate(j + 1)
-                finish(j, HALF, I)
-            else:
-                centre(j, HALF, HALF + QUARTER)
-                finish(j, 0, HALF)
-                centre(j, HALF + QUARTER, I)
-                finish(j, HALF, HALF + QUARTER)
-                finish(j, HALF + QUARTER, I)
+                inverse_spread(j + 1)
+            finish(j, HALF, I)

from contextlib import ExitStack

import concourse.mybir as mybir
from concourse.masks import make_identity

K, L, Q, I = 512, 1024, 512, 1024
FLOPS = 2 * Q * I * (K + L)

F32 = mybir.dt.float32
BF16 = mybir.dt.bfloat16
I32 = mybir.dt.int32
U32 = mybir.dt.uint32
U8 = mybir.dt.uint8
FP8X4 = mybir.dt.float8_e4m3fn_x4
FP4X4 = mybir.dt.float4_e2m1fn_x4
ACT = mybir.ActivationFunctionType
ALU = mybir.AluOpType

P = 128
HALF = 512
QUARTER = 256
ROW_TILES = Q // P
L_PASSES = L // 512
EPS = 0.02
SCALAR_COLS = 64
QA_ROW = 4


def tile_mix_scores_of_two_sources_levelled_kernel(
    tc, qa_words, qa_scales, ka, qb_words, qb_scales, kb_words, kb_scales, gn, bi, out
):
    nc = tc.nc
    with ExitStack() as ctx:
        sb = ctx.enter_context(tc.tile_pool(name="sb", bufs=1))
        ps = ctx.enter_context(tc.psum_pool(name="ps", bufs=1))
        ctx.enter_context(tc.manual_schedule())

        def tile(name, shape, dtype):
            return sb.tile(shape, dtype, name=name, align_bytes=64)

        def bank(name, tag):
            return ps.tile([P, HALF], F32, name=name, tag=tag)

        def halves(h):
            return slice(h * HALF, (h + 1) * HALF)

        ident = tile("ident", [P, P], F32)

        kb_plane = tile("kb_plane", [P, L_PASSES, I], U8)
        qb_plane = tile("qb_plane", [P, L_PASSES, Q], U8)
        qa_plane = tile("qa_plane", [P, 1, Q], U8)
        nc.vector.memset(kb_plane[:].bitcast(I32), 0)
        for plane in (qb_plane, qa_plane):
            nc.vector.memset(plane[:].bitcast(I32), 0)
        stats = [tile("stats%d" % j, [P, 12], F32) for j in range(ROW_TILES)]
        for j in range(1, ROW_TILES):
            nc.vector.memset(stats[j][:], float(HALF))
        warm = tile("warm", [P, 1], F32)
        nc.vector.memset(warm[:], 1.0)

        def load_plane(engine, plane, scales, first=0):
            for r in range(4):
                engine.dma_start(
                    out=plane[first + r : P : 32].bitcast(I32),
                    in_=scales[:, r:16:4, :].rearrange("g s n -> s g n").bitcast(I32),
                )

        def load_kb(h, first, count):
            t = tile("kb%d%d" % (h, first), [P, count, 4 * HALF], U8)
            src = kb_words.rearrange("g p n t -> p g (n t)")[:, first : first + count, 4 * HALF * h : 4 * HALF * (h + 1)]
            nc.sync.dma_start(out=t[:].bitcast(I32), in_=src.bitcast(I32))
            for g in range(count):
                kb[h, first + g] = t[:, g, :]

        def load_qb(v):
            t = tile("qb%d" % v, [P, L_PASSES, Q], U8)
            src = qb_words.rearrange("g p n -> p g n")[:, :, Q * v : Q * (v + 1)]
            nc.sync.dma_start(out=t[:].bitcast(I32), in_=src.bitcast(I32))
            return t

        def load_qa(v):
            t = tile("qa%d" % v, [P, 2 * Q], U8)
            src = qa_words[0].rearrange("p n t -> p (n t)")[:, 2 * Q * v : 2 * Q * (v + 1)]
            nc.sync.dma_start(out=t[:].bitcast(I32), in_=src.bitcast(I32))
            return t

        def load_ka(lo, hi):
            t = tile("ka%d" % lo, [P, 4, hi - lo], F32)
            nc.sync.dma_start(out=t[:], in_=ka.rearrange("(p t) i -> p t i", t=4)[:, :, lo:hi])
            return t

        blocks = I // P
        gn_cols = tile("gn_cols", [P, blocks], F32)
        bi_cols = tile("bi_cols", [P, blocks], F32)
        nc.scalar.dma_start(out=gn_cols[:], in_=gn.rearrange("o (p c) -> (o p) c", p=P))
        nc.scalar.dma_start(out=bi_cols[:], in_=bi.rearrange("o (p c) -> (o p) c", p=P))
        make_identity(nc, ident[:])
        kb = {}
        qb = [load_qb(0)]
        load_kb(0, 0, L_PASSES)
        load_plane(nc.sync, kb_plane, kb_scales)
        ka_first = load_ka(0, HALF)
        load_plane(nc.sync, qb_plane, qb_scales)
        ka_third = load_ka(HALF, HALF + QUARTER)
        ka_last = load_ka(HALF + QUARTER, I)
        qa = [load_qa(0)]
        load_plane(nc.gpsimd, qa_plane, qa_scales, QA_ROW)
        load_kb(1, 0, 1)
        load_kb(1, 1, 1)
        qb.append(load_qb(1))
        qa.append(load_qa(1))

        warm_out = tile("warm_out", [P, 1], F32)
        nc.scalar.activation(out=warm_out[:], in_=warm[:], func=ACT.Abs_reciprocal_sqrt)

        def spread(name, cols, first_bank):
            banks = [bank("%s%d" % (name, u), "bank%d" % (first_bank + u)) for u in range(2)]
            for c in range(blocks):
                nc.tensor.transpose(
                    banks[c // 4][:, (c % 4) * P : (c % 4 + 1) * P],
                    cols[:, c : c + 1].to_broadcast([P, P]),
                    ident[:],
                )
            return banks

        def gather(name, banks):
            full = tile(name, [P, I], F32)
            for u in range(2):
                nc.scalar.copy(
                    out=full[:].rearrange("p (n c) -> p n c", c=blocks)[:, :, 4 * u : 4 * u + 4],
                    in_=banks[u][:].rearrange("p (c n) -> p n c", c=4),
                )
            return full

        gn_sb = gather("gn_sb", spread("gn_ps", gn_cols, 2))
        bi_sb = gather("bi_sb", spread("bi_ps", bi_cols, 6))

        ka_codes = [tile("ka_codes%d" % h, [P, HALF], U32) for h in range(2)]
        ka_plane = [tile("ka_plane%d" % h, [P, HALF], U8) for h in range(2)]
        grouped = {(h, u): tile("grouped%d%d" % (h, u), [P, QUARTER, 4], BF16) for h in range(2) for u in range(2)}

        def interleave(copy, dst, raw):
            copy(out=dst.rearrange("p (c n) t -> p c t n", n=4), in_=raw.rearrange("p t (c n) -> p c t n", n=4))

        def quantise(h, u):
            cols = slice(u * QUARTER, (u + 1) * QUARTER)
            nc.vector.quantize_mx(
                out=ka_codes[h][:, cols].bitcast(FP8X4),
                scales=ka_plane[h][:, cols],
                in_=grouped[h, u][:].rearrange("p n t -> p (n t)"),
            )

        acc = {}

        def b_pass(j, h, g, start=False, stop=False):
            nc.tensor.matmul_mx(
                out=acc[j, h][:],
                lhsT=qb[j // 2][:, g, 2 * P * (j % 2) : 2 * P * (j % 2 + 1)].bitcast(FP4X4),
                lhsT_scale=qb_plane[:, g, P * j : P * (j + 1)],
                rhs=kb[h, g].bitcast(FP8X4),
                rhs_scale=kb_plane[:, g, halves(h)],
                start=start,
                stop=stop,
            )

        def a_pass(j, h, stop=False):
            nc.tensor.matmul_mx(
                out=acc[j, h][:],
                lhsT=qa[j // 2][:, 4 * P * (j % 2) : 4 * P * (j % 2 + 1)].bitcast(FP8X4),
                lhsT_scale=qa_plane[QA_ROW:, 0, P * j : P * (j + 1)],
                rhs=ka_codes[h][:].bitcast(FP8X4),
                rhs_scale=ka_plane[h][:],
                start=False,
                stop=stop,
            )

        def scores(j, h):
            acc[j, h] = bank("acc%d%d" % (j, h), "bank%d" % (4 * h + j))
            b_pass(j, h, 0, start=True)
            if h == 0:
                b_pass(j, h, 1)
                a_pass(j, h, stop=True)
            else:
                a_pass(j, h)
                b_pass(j, h, 1, stop=True)

        filled = [0] * ROW_TILES
        places = {}

        def stats_vector(j, h):
            at = filled[j]
            filled[j] = at + 6
            nc.vector.bn_stats(out=stats[j][:, at : at + 6], in_=acc[j, h][:])

        def mean_scalar(j, h):
            at = filled[j]
            filled[j] = at + 3
            places[j, h] = at
            unused = tile("unused_a%d%d" % (j, h), [P, HALF], BF16)
            nc.scalar.activation(
                out=unused[:], in_=acc[j, h][:], func=ACT.Identity, scale=1.0 / HALF,
                accum_out=stats[j][:, at + 1 : at + 2],
            )

        def spread_scalar(j, h):
            at = places[j, h]
            unused = tile("unused_b%d%d" % (j, h), [P, HALF], BF16)
            nc.scalar.activation(
                out=unused[:], in_=acc[j, h][:], func=ACT.Square, scale=-1.0,
                bias=stats[j][:, at + 1 : at + 2], accum_out=stats[j][:, at + 2 : at + 3],
            )

        for j in range(2):
            acc[j, 0] = bank("acc%d0" % j, "bank%d" % j)
            b_pass(j, 0, 0, start=True)
            b_pass(j, 0, 1)

        interleave(nc.vector.tensor_copy, grouped[0, 0][:], ka_first[:, :, :QUARTER])
        interleave(nc.scalar.copy, grouped[0, 1][:], ka_first[:, :, QUARTER:])
        quantise(0, 0)
        quantise(0, 1)
        for j in range(2):
            a_pass(j, 0, stop=True)

        interleave(nc.scalar.copy, grouped[1, 0][:], ka_third[:])
        cut = QUARTER - SCALAR_COLS
        interleave(nc.vector.tensor_copy, grouped[1, 1][:, :cut, :], ka_last[:, :, :cut])
        interleave(nc.scalar.copy, grouped[1, 1][:, cut:, :], ka_last[:, :, cut:])
        quantise(1, 0)
        quantise(1, 1)
        stats_vector(0, 0)
        mean_scalar(1, 0)
        spread_scalar(1, 0)

        scores(0, 1)
        scores(1, 1)
        for j in range(2, ROW_TILES):
            scores(j, 0)
            scores(j, 1)

        mv = [tile("mv%d" % j, [P, 2], F32) for j in range(ROW_TILES)]
        rstd = [tile("rstd%d" % j, [P, 1], F32) for j in range(ROW_TILES)]
        centred = [tile("centred%d" % j, [P, I], F32) for j in range(ROW_TILES)]
        res = [tile("res%d" % j, [P, I], F32) for j in range(ROW_TILES)]

        def aggregate(j):
            nc.vector.bn_aggr(out=mv[j][:], in_=stats[j][:, : filled[j]])

        def inverse_spread(j):
            nc.scalar.activation(out=rstd[j][:], in_=mv[j][:, 1:2], func=ACT.Abs_reciprocal_sqrt, bias=EPS)

        def centre(j, lo, hi):
            h = lo // HALF
            nc.vector.scalar_tensor_tensor(
                out=centred[j][:, lo:hi], in0=acc[j, h][:, lo - h * HALF : hi - h * HALF], scalar=mv[j][:, 0:1],
                in1=gn_sb[:, lo:hi], op0=ALU.subtract, op1=ALU.mult,
            )

        def finish(j, lo, hi):
            nc.vector.scalar_tensor_tensor(
                out=res[j][:, lo:hi], in0=centred[j][:, lo:hi], scalar=rstd[j][:],
                in1=bi_sb[:, lo:hi], op0=ALU.mult, op1=ALU.add,
            )
            nc.sync.dma_start(out=out[j * P : (j + 1) * P, lo:hi], in_=res[j][:, lo:hi])

        stats_vector(0, 1)
        aggregate(0)
        stats_vector(1, 1)
        inverse_spread(0)
        centre(0, 0, HALF)
        aggregate(1)
        mean_scalar(2, 0)
        inverse_spread(1)
        mean_scalar(2, 1)
        spread_scalar(2, 0)
        spread_scalar(2, 1)
        centre(0, HALF, I)
        finish(0, 0, HALF)
        finish(0, HALF, I)
        mean_scalar(3, 0)
        mean_scalar(3, 1)
        for j in range(1, ROW_TILES):
            centre(j, 0, HALF)
            centre(j, HALF, I)
            finish(j, 0, HALF)
            if j == 2:
                spread_scalar(3, 0)
                spread_scalar(3, 1)
            if j + 1 < ROW_TILES:
                aggregate(j + 1)
                inverse_spread(j + 1)
            finish(j, HALF, I)
